import numpy as np
import ml_dtypes


def mxq(x, axis, fmt="e4m3"):
    dtype, down = {"e4m3": (ml_dtypes.float8_e4m3fn, 7), "e5m2": (ml_dtypes.float8_e5m2, 14)}[fmt]
    v = np.moveaxis(np.asarray(x, np.float32).astype(ml_dtypes.bfloat16).astype(np.float64), axis, -1)
    blocks = v.reshape(v.shape[:-1] + (-1, 32))
    amax = np.abs(blocks).max(-1, keepdims=True)
    byte = np.maximum(np.where(amax > 0, np.frexp(amax)[1] - 1 + 127, 0) - down, 1)
    scale = np.exp2(byte - 127.0)
    codes = (blocks / scale).astype(np.float32).astype(dtype).astype(np.float64)
    return np.moveaxis((codes * scale).reshape(v.shape), -1, axis)


WIDE = False


def mx_kscale(k):
    if not WIDE:
        return np.ones(k)
    levels = np.array([10, -10, 5, -5, 0])
    if k % 512:
        return np.exp2(np.random.permutation(np.resize(levels, k // 32))).repeat(32)
    a = np.empty((k // 512, 16))
    for p in range(k // 512):
        a[p, :8] = np.random.permutation(np.resize(levels, 8))
        for g in range(8):
            far = levels[np.abs(levels - a[p, g]) >= 10]
            a[p, g + 8] = far[np.random.randint(len(far))]
    return np.exp2(a.ravel()).repeat(32)


def f64(x):
    return np.asarray(x).astype(np.float64)


def striped(idx):
    return np.tile(idx.reshape(-1, 16).T, (8, 1)).astype(np.uint16)


def unstriped(offs):
    return offs[:16].T.reshape(-1).astype(np.int64)


E2M1 = np.array([0.0, 0.5, 1.0, 1.5, 2.0, 3.0, 4.0, 6.0, -0.0, -0.5, -1.0, -1.5, -2.0, -3.0, -4.0, -6.0])


def pack_weight(w, fmt):
    k, n = w.shape
    w = f64(np.asarray(w, np.float32).astype(ml_dtypes.bfloat16)).reshape(k // 32, 32, n)
    amax = np.abs(w).max(1)
    if fmt == "e4m3":
        byte = np.frexp(amax)[1] - 1 + 127 - 7
    else:
        mant, ex = np.frexp(amax / 6.0)
        byte = np.where(mant > 0.5, ex, ex - 1) + 127
    byte = np.clip(np.where(amax > 0, byte, 1), 1, 254)
    scaled = (w * np.exp2(127.0 - byte)[:, None, :]).reshape(k, n).astype(np.float32)
    by_word = np.ascontiguousarray(scaled.reshape(k // 512, 128, 4, n).transpose(0, 1, 3, 2))
    if fmt == "e4m3":
        words = by_word.astype(ml_dtypes.float8_e4m3fn).view(np.uint8)
    else:
        c = by_word.astype(ml_dtypes.float4_e2m1fn).view(np.uint8) & 0xF
        words = (c[..., 0::2] | (c[..., 1::2] << 4)).reshape(k // 512, 128, 2 * n)
    return np.ascontiguousarray(words), np.ascontiguousarray(byte.astype(np.uint8).reshape(k // 512, 16, n))


def unpack_weight(words, scales, fmt):
    g, _, n = scales.shape
    words = np.ascontiguousarray(words).reshape(g, 128, n, -1)
    if fmt == "e4m3":
        vals = words.view(ml_dtypes.float8_e4m3fn).astype(np.float64)
    else:
        nib = np.empty((g, 128, n, 4), np.uint8)
        nib[..., 0::2] = words & 0xF
        nib[..., 1::2] = words >> 4
        vals = E2M1[nib]
    vals = vals * np.repeat(np.exp2(scales.astype(np.float64) - 127.0), 8, axis=1)[..., None]
    return vals.transpose(0, 1, 3, 2).reshape(g * 512, n)


def gelu(v):
    return 0.5 * v * (1.0 + np.tanh(np.sqrt(2.0 / np.pi) * (v + 0.044715 * v**3)))


K, T, S, H, T2, P = 1536, 4096, 1024, 1024, 2048, 512


def setup_inputs():
    n = np.random.standard_normal
    s = mx_kscale(K)[:, None]
    u = mx_kscale(H)[:, None]
    d = {}
    d["tab_words"], d["tab_scales"] = pack_weight(n((K, T)) * s, "e4m3")
    d["offs"] = striped(np.random.permutation(T)[:S])
    d["w1"] = (n((K, H)) / K ** 0.5 / s * u.T).astype(np.float32)
    d["fresh"] = (n((H, S)) * u).astype(np.float32)
    d["wgs"] = np.exp(0.3 * n((128, S))).astype(np.float32)
    d["page0"] = (n((H, T2)) * u).astype(np.float32)
    d["offs2"] = striped(np.random.permutation(T2)[:S])
    d["offs3"] = striped(np.random.permutation(T2)[:P])
    d["expo"] = (np.exp(0.3 * n((H, 1))) * n((H, P))).astype(np.float32)
    d["w4_words"], d["w4_scales"] = pack_weight(n((H, H)) / H ** 0.5 / u, "e2m1")
    d["offs4"] = striped(np.random.permutation(T2)[:P])
    d["gref"] = (1.2 * n(H) / u[:, 0]).astype(np.float32)
    return d


def reference(tab_words, tab_scales, offs, w1, fresh, wgs, page0, offs2, offs3,
              expo, w4_words, w4_scales, offs4, gref):
    v = unpack_weight(tab_words, tab_scales, "e4m3")[:, unstriped(offs)]
    h = np.abs((mxq(f64(w1), 0, "e4m3").T @ v) - f64(fresh))
    page = f64(page0).copy()
    page[:, unstriped(offs2)] = np.tile(f64(wgs), (H // 128, 1)) * h
    x = page[:, unstriped(offs3)] * f64(expo)
    w4 = unpack_weight(w4_words, w4_scales, "e2m1")
    y = w4.T @ mxq(x, 0, "e4m3")
    ref = page[:, unstriped(offs4)] * f64(gref)[:, None]
    return y / (1.0 + np.abs(ref))

@@ -1,0 +1,259 @@
+from contextlib import ExitStack
+
+import concourse.mybir as mybir
+
+K, T, S, H, T2, M = 1536, 4096, 1024, 1024, 2048, 512
+FLOPS = 2 * K * H * S + 2 * H * H * M
+
+F32 = mybir.dt.float32
+BF16 = mybir.dt.bfloat16
+I32 = mybir.dt.int32
+U32 = mybir.dt.uint32
+U16 = mybir.dt.uint16
+U8 = mybir.dt.uint8
+FP8X4 = mybir.dt.float8_e4m3fn_x4
+FP4X4 = mybir.dt.float4_e2m1fn_x4
+ACT = mybir.ActivationFunctionType
+ALU = mybir.AluOpType
+
+P = 128
+PACK = 4
+PASS = P * PACK
+BANK = 512
+K_PASSES = K // PASS
+R_PASSES = H // PASS
+TILES = H // P
+QUADS = 4
+LIST_COLS = 16
+
+
+def tile_list_paint_panel_rating_kernel(
+    tc, tab_words, tab_scales, offs, w1, fresh, wgs, page0, offs2, offs3,
+    expo, w4_words, w4_scales, offs4, gref, out,
+):
+    nc = tc.nc
+
+    def dealt(rows):
+        return rows.rearrange("(b p i) c -> b i p c", b=R_PASSES, i=PACK)
+
+    fresh_rows, page_rows, expo_rows, out_rows = dealt(fresh), dealt(page0), dealt(expo), dealt(out)
+    wgs_rows = wgs.rearrange("(q i) j -> q i j", i=PACK)
+
+    with ExitStack() as ctx:
+        lists = ctx.enter_context(tc.tile_pool(name="lists", bufs=1))
+        keep = ctx.enter_context(tc.tile_pool(name="keep", bufs=1))
+        shared = ctx.enter_context(tc.tile_pool(name="shared", bufs=1))
+        psum = ctx.enter_context(tc.psum_pool(name="psum", bufs=1))
+
+        def tiles(name, count, shape, dtype):
+            return [keep.tile(shape, dtype, name=f"{name}{n}", align_bytes=64) for n in range(count)]
+
+        idx = lists.tile([P, S // LIST_COLS], U16, name="idx")
+        idx2 = lists.tile([P, S // LIST_COLS], U16, name="idx2")
+        idx3 = lists.tile([P, M // LIST_COLS], U16, name="idx3")
+        idx4 = lists.tile([P, M // LIST_COLS], U16, name="idx4")
+
+        table = [shared.tile([P, T], U32, name=f"table{a}", offset=4 * T * a) for a in range(K_PASSES)]
+        own_pages = TILES - 2 * K_PASSES
+        page = tiles("page", own_pages, [P, T2], F32)
+        table_scales = keep.tile([P, T], U8, align_bytes=64)
+        picked = tiles("picked", K_PASSES, [P, S], U32)
+        picked_scales = keep.tile([P, S], U8, align_bytes=64)
+        w1_raw = tiles("w1_raw", K_PASSES, [P, PACK, PASS], F32)
+        w1_grouped = tiles("w1_grouped", 2, [P, PACK * PASS], BF16)
+        w1_codes = tiles("w1_codes", R_PASSES * K_PASSES, [P, PASS], U32)
+        w1_scales = tiles("w1_scales", R_PASSES * K_PASSES, [P, PASS], U8)
+        gain_first = keep.tile([P, S], F32, align_bytes=64)
+        gain_rest = keep.tile([P, PACK - 1, S], F32, align_bytes=64)
+        dist = tiles("dist", TILES, [P, S], F32)
+        exposure = tiles("exposure", PACK, [P, M], F32)
+        x_rows = tiles("x_rows", 2, [P, PACK, M // 2], F32)
+        x_grouped = tiles("x_grouped", 2, [P, PACK * M // 2], BF16)
+        x_codes = tiles("x_codes", R_PASSES, [P, M], U32)
+        x_scales = tiles("x_scales", R_PASSES, [P, M], U8)
+        damp = tiles("damp", TILES, [P, M], F32)
+        w4_raw = tiles("w4_raw", R_PASSES, [P, 2 * H], U8)
+        w4_codes = tiles("w4_codes", R_PASSES, [P, 2 * H], U8)
+        w4_scales_raw = keep.tile([P, R_PASSES, H], U8, align_bytes=64)
+        w4_planes = keep.tile([P, R_PASSES, H], U8, align_bytes=64)
+        ref_gain = keep.tile([P, R_PASSES, PACK], F32, align_bytes=64)
+        banks = [psum.tile([P, BANK], F32, name=f"bank{n}") for n in range(8)]
+
+        def load_w1(b, a):
+            rows = w1[PASS * a : PASS * (a + 1), PASS * b : PASS * (b + 1)]
+            nc.sync.dma_start(out=w1_raw[a][:], in_=rows.rearrange("(p t) c -> p t c", t=PACK))
+
+        def quantize_w1(b, a):
+            grouped = w1_grouped[(K_PASSES * b + a) % 2]
+            nc.scalar.copy(
+                out=grouped[:].rearrange("p (i m t) -> p m t i", i=PACK, t=PACK),
+                in_=w1_raw[a][:].rearrange("p t (m i) -> p m t i", i=PACK),
+            )
+            n = K_PASSES * b + a
+            nc.vector.quantize_mx(out=w1_codes[n][:].bitcast(FP8X4), scales=w1_scales[n][:], in_=grouped[:])
+
+        def load_fresh(t):
+            nc.sync.dma_start(out=dist[t][:], in_=fresh_rows[t // PACK, t % PACK])
+
+        def load_page(t):
+            if t >= own_pages:
+                page.append(shared.tile([P, T2], F32, name=f"page{t}", offset=4 * T2 * (t - own_pages)))
+            nc.sync.dma_start(out=page[t][:], in_=page_rows[t // PACK, t % PACK])
+
+        def load_expo(t):
+            nc.sync.dma_start(out=exposure[t % PACK][:], in_=expo_rows[t // PACK, t % PACK])
+
+        def distances(t):
+            b, i = divmod(t, PACK)
+            rows = slice(P * i, P * (i + 1))
+            for half in range(S // BANK):
+                cols = slice(BANK * half, BANK * (half + 1))
+                bank = banks[(2 * t + half) % len(banks)]
+                for a in range(K_PASSES):
+                    n = K_PASSES * b + a
+                    nc.tensor.matmul_mx(
+                        out=bank[:],
+                        lhsT=w1_codes[n][:, rows].bitcast(FP8X4),
+                        lhsT_scale=w1_scales[n][:, rows],
+                        rhs=picked[a][:, cols].bitcast(FP8X4),
+                        rhs_scale=picked_scales[PACK * a : P, cols],
+                        start=(a == 0),
+                        stop=(a == K_PASSES - 1),
+                    )
+                nc.vector.tensor_tensor(out=dist[t][:, cols], in0=bank[:], in1=dist[t][:, cols], op=ALU.subtract)
+                nc.scalar.activation(out=dist[t][:, cols], in_=dist[t][:, cols], func=ACT.Abs)
+
+        def put(t, pieces):
+            i = t % PACK
+            width = S // pieces
+            for piece in range(pieces):
+                cols = slice(width * piece, width * (piece + 1))
+                entries = idx2[:, width // LIST_COLS * piece : width // LIST_COLS * (piece + 1)]
+                gain = gain_first[:, cols] if i == 0 else gain_rest[:, i - 1, cols]
+                nc.vector.tensor_tensor(out=page[t][:].indirect(entries), in0=dist[t][:, cols], in1=gain, op=ALU.mult)
+
+        def fetch_x(t):
+            i = t % PACK
+            width = M // 2
+            for half in range(2):
+                entries = idx3[:, width // LIST_COLS * half : width // LIST_COLS * (half + 1)]
+                nc.vector.tensor_tensor(
+                    out=x_rows[half][:, i, :],
+                    in0=page[t][:].indirect(entries),
+                    in1=exposure[i][:, width * half : width * (half + 1)],
+                    op=ALU.mult,
+                )
+
+        def fetch_ref(t):
+            b, i = divmod(t, PACK)
+            nc.vector.tensor_copy(out=damp[t][:], in_=page[t][:].indirect(idx4[:]))
+            nc.scalar.activation(out=damp[t][:], in_=damp[t][:], func=ACT.Abs, scale=ref_gain[:, b, i : i + 1])
+            nc.scalar.activation(out=damp[t][:], in_=damp[t][:], func=ACT.Abs_reciprocal_sqrt, bias=1.0)
+            nc.scalar.activation(out=damp[t][:], in_=damp[t][:], func=ACT.Square)
+
+        def quantize_x(b):
+            width = M // 2
+            for half in range(2):
+                views = dict(
+                    out=x_grouped[half][:].rearrange("p (c e i) -> p c i e", e=4, i=PACK),
+                    in_=x_rows[half][:].rearrange("p i (c e) -> p c i e", e=4),
+                )
+                if b == R_PASSES - 1 and half == 1:
+                    nc.vector.tensor_copy(**views)
+                else:
+                    nc.scalar.copy(**views)
+            for half in range(2):
+                cols = slice(width * half, width * (half + 1))
+                nc.vector.quantize_mx(
+                    out=x_codes[b][:, cols].bitcast(FP8X4), scales=x_scales[b][:, cols], in_=x_grouped[half][:]
+                )
+
+        def rate(t, b):
+            nc.tensor.matmul_mx(
+                out=banks[t][:],
+                lhsT=w4_codes[b][:, 2 * P * t : 2 * P * (t + 1)].bitcast(FP4X4),
+                lhsT_scale=w4_planes[:, b, P * t : P * (t + 1)],
+                rhs=x_codes[b][:].bitcast(FP8X4),
+                rhs_scale=x_scales[b][:],
+                start=(b == 0),
+                stop=(b == R_PASSES - 1),
+            )
+
+        nc.vector.memset(table_scales[:].bitcast(I32), 0)
+        nc.vector.memset(w4_scales_raw[:].bitcast(I32), 0)
+        nc.sync.dma_start(out=idx[:], in_=offs)
+        for a in range(K_PASSES):
+            load_w1(0, a)
+            if a == 0:
+                for q in range(QUADS):
+                    nc.sync.dma_start(
+                        out=table_scales[32 * q : 32 * q + PACK * K_PASSES, :].bitcast(I32),
+                        in_=tab_scales[:, PACK * q : PACK * (q + 1), :].bitcast(I32),
+                    )
+                for q in range(QUADS):
+                    nc.sync.dma_start(
+                        out=w4_scales_raw[32 * q : 32 * q + PACK, :, :].bitcast(I32),
+                        in_=w4_scales[:, PACK * q : PACK * (q + 1), :].rearrange("a r n -> r a n").bitcast(I32),
+                    )
+            nc.sync.dma_start(
+                out=table[a][:].bitcast(I32), in_=tab_words[a].rearrange("p t i -> p (t i)").bitcast(I32)
+            )
+        nc.sync.dma_start(out=idx2[:], in_=offs2)
+        load_fresh(0)
+        for q in range(QUADS):
+            nc.sync.dma_start(out=gain_first[32 * q : 32 * (q + 1), :], in_=wgs_rows[:, 0, :])
+        load_page(0)
+        load_fresh(1)
+        nc.sync.dma_start(out=idx3[:], in_=offs3)
+        nc.sync.dma_start(out=idx4[:], in_=offs4)
+        load_expo(0)
+        nc.sync.dma_start(out=ref_gain[:], in_=gref.rearrange("(b p i) -> p b i", b=R_PASSES, i=PACK))
+        for q in range(QUADS):
+            nc.sync.dma_start(out=gain_rest[32 * q : 32 * (q + 1), :, :], in_=wgs_rows[:, 1:PACK, :])
+
+        nc.vector.tensor_copy(out=picked_scales[:], in_=table_scales[:].indirect(idx[:]))
+        nc.vector.tensor_copy(
+            out=w4_planes[:].rearrange("p a (b i q) -> p (a b) q i", b=R_PASSES, i=PACK),
+            in_=w4_scales_raw[:].rearrange("p a (b q i) -> p (a b) q i", b=R_PASSES, i=PACK),
+        )
+        for a in range(K_PASSES):
+            quantize_w1(0, a)
+            pieces = 2 if a == K_PASSES - 1 else 1
+            width = S // pieces
+            for piece in range(pieces):
+                entries = idx[:, width // LIST_COLS * piece : width // LIST_COLS * (piece + 1)]
+                nc.vector.tensor_copy(
+                    out=picked[a][:, width * piece : width * (piece + 1)], in_=table[a][:].indirect(entries)
+                )
+
+        distances(0)
+        for t in range(TILES):
+            if t + 1 < TILES:
+                if t + 2 < TILES:
+                    load_fresh(t + 2)
+                load_page(t + 1)
+                if t < K_PASSES:
+                    load_w1(1, t)
+                    quantize_w1(1, t)
+                if t == K_PASSES:
+                    for b in range(R_PASSES):
+                        nc.sync.dma_start(out=w4_raw[b][:].bitcast(I32), in_=w4_words[b].bitcast(I32))
+                        nc.scalar.copy(
+                            out=w4_codes[b][:].bitcast(U16).rearrange("p (b i q) -> p b q i", b=R_PASSES, i=PACK),
+                            in_=w4_raw[b][:].bitcast(U16).rearrange("p (b q i) -> p b q i", b=R_PASSES, i=PACK),
+                        )
+                distances(t + 1)
+            put(t, 2 if t == 0 else 1)
+            fetch_x(t)
+            if t + 1 < TILES:
+                load_expo(t + 1)
+            if t % PACK == PACK - 1:
+                quantize_x(t // PACK)
+            fetch_ref(t)
+
+        for b in range(R_PASSES):
+            for t in range(TILES):
+                rate(t, b)
+                if b == R_PASSES - 1:
+                    nc.vector.tensor_tensor(out=damp[t][:], in0=banks[t][:], in1=damp[t][:], op=ALU.mult)
+                    nc.sync.dma_start(out=out_rows[t // PACK, t % PACK], in_=damp[t][:])

@@ -1,6 +1,7 @@
 from contextlib import ExitStack
 
 import concourse.mybir as mybir
+from concourse.masks import make_identity
 
 K, T, S, H, T2, M = 1536, 4096, 1024, 1024, 2048, 512
 FLOPS = 2 * K * H * S + 2 * H * H * M
@@ -25,6 +26,7 @@ R_PASSES = H // PASS
 TILES = H // P
 QUADS = 4
 LIST_COLS = 16
+CHUNK = 2 * P
 
 
 def tile_list_paint_panel_rating_kernel(
@@ -33,10 +35,11 @@ def tile_list_paint_panel_rating_kernel(
 ):
     nc = tc.nc
 
-    def dealt(rows):
-        return rows.rearrange("(b p i) c -> b i p c", b=R_PASSES, i=PACK)
+    def tile_rows(matrix, t):
+        if t < PACK:
+            return matrix[P * t : P * (t + 1), :]
+        return matrix[PASS:, :].rearrange("(p i) c -> i p c", i=PACK)[t - PACK]
 
-    fresh_rows, page_rows, expo_rows, out_rows = dealt(fresh), dealt(page0), dealt(expo), dealt(out)
     wgs_rows = wgs.rearrange("(q i) j -> q i j", i=PACK)
 
     with ExitStack() as ctx:
@@ -54,85 +57,132 @@ def tile_list_paint_panel_rating_kernel(
         idx4 = lists.tile([P, M // LIST_COLS], U16, name="idx4")
 
         table = [shared.tile([P, T], U32, name=f"table{a}", offset=4 * T * a) for a in range(K_PASSES)]
-        own_pages = TILES - 2 * K_PASSES
-        page = tiles("page", own_pages, [P, T2], F32)
+        page_slots = [6, 7, 0, 1, 3, 6, 7, 0]
+        page = []
         table_scales = keep.tile([P, T], U8, align_bytes=64)
         picked = tiles("picked", K_PASSES, [P, S], U32)
         picked_scales = keep.tile([P, S], U8, align_bytes=64)
         w1_raw = tiles("w1_raw", K_PASSES, [P, PACK, PASS], F32)
-        w1_grouped = tiles("w1_grouped", 2, [P, PACK * PASS], BF16)
-        w1_codes = tiles("w1_codes", R_PASSES * K_PASSES, [P, PASS], U32)
-        w1_scales = tiles("w1_scales", R_PASSES * K_PASSES, [P, PASS], U8)
-        gain_first = keep.tile([P, S], F32, align_bytes=64)
-        gain_rest = keep.tile([P, PACK - 1, S], F32, align_bytes=64)
+        w1_grouped = keep.tile([P, 2 * PACK * PASS], BF16, align_bytes=64)
+        widths = (CHUNK, CHUNK, PASS)
+        w1_codes = [keep.tile([P, K_PASSES * w], U32, name=f"w1_codes{n}", align_bytes=64) for n, w in enumerate(widths)]
+        w1_scales = [keep.tile([P, K_PASSES * w], U8, name=f"w1_scales{n}", align_bytes=64) for n, w in enumerate(widths)]
+        gain_plain = keep.tile([P, S], F32, align_bytes=64)
+        gain_dealt = []
+        identity = keep.tile([P, P], F32, align_bytes=64)
+        gref_rows = keep.tile([P, P], F32, align_bytes=64)
+        staged = keep.tile([P, 2 * BANK], F32, align_bytes=64)
+        negated = [staged[:, BANK * half : BANK * (half + 1)] for half in range(2)]
+        turned = tiles("turned", 2, [P, BANK], F32)
         dist = tiles("dist", TILES, [P, S], F32)
-        exposure = tiles("exposure", PACK, [P, M], F32)
+        exposure = tiles("exposure", TILES, [P, M], F32)
+        x_plain = tiles("x_plain", PACK, [P, M], F32)
         x_rows = tiles("x_rows", 2, [P, PACK, M // 2], F32)
-        x_grouped = tiles("x_grouped", 2, [P, PACK * M // 2], BF16)
-        x_codes = tiles("x_codes", R_PASSES, [P, M], U32)
+        x_codes = {1: keep.tile([P, M], U32, name="x_codes1", align_bytes=64)}
         x_scales = tiles("x_scales", R_PASSES, [P, M], U8)
         damp = tiles("damp", TILES, [P, M], F32)
         w4_raw = tiles("w4_raw", R_PASSES, [P, 2 * H], U8)
-        w4_codes = tiles("w4_codes", R_PASSES, [P, 2 * H], U8)
+        w4_codes = tiles("w4_codes", R_PASSES, [P, 2 * PASS], U8)
         w4_scales_raw = keep.tile([P, R_PASSES, H], U8, align_bytes=64)
-        w4_planes = keep.tile([P, R_PASSES, H], U8, align_bytes=64)
-        ref_gain = keep.tile([P, R_PASSES, PACK], F32, align_bytes=64)
+        w4_planes = keep.tile([P, R_PASSES, PASS], U8, align_bytes=64)
+        ref_gain = tiles("ref_gain", R_PASSES, [P, PACK], F32)
         banks = [psum.tile([P, BANK], F32, name=f"bank{n}") for n in range(8)]
 
-        def load_w1(b, a):
-            rows = w1[PASS * a : PASS * (a + 1), PASS * b : PASS * (b + 1)]
-            nc.sync.dma_start(out=w1_raw[a][:], in_=rows.rearrange("(p t) c -> p t c", t=PACK))
+        def load_w1(a, first, width):
+            rows = w1[PASS * a : PASS * (a + 1), first : first + width]
+            cols = slice(first % PASS, first % PASS + width)
+            nc.sync.dma_start(out=w1_raw[a][:, :, cols], in_=rows.rearrange("(p t) c -> p t c", t=PACK))
 
-        def quantize_w1(b, a):
-            grouped = w1_grouped[(K_PASSES * b + a) % 2]
-            nc.scalar.copy(
-                out=grouped[:].rearrange("p (i m t) -> p m t i", i=PACK, t=PACK),
-                in_=w1_raw[a][:].rearrange("p t (m i) -> p m t i", i=PACK),
+        def group_w1(chunk, a, grouped):
+            if chunk < 2:
+                cols = slice(CHUNK * chunk, CHUNK * (chunk + 1))
+                nc.scalar.copy(
+                    out=grouped.rearrange("p (c e t) -> p c t e", e=4, t=PACK),
+                    in_=w1_raw[a][:, :, cols].rearrange("p t (c e) -> p c t e", e=4),
+                )
+            else:
+                nc.scalar.copy(
+                    out=grouped.rearrange("p (i m t) -> p m i t", i=PACK, t=PACK),
+                    in_=w1_raw[a][:].rearrange("p t (m i) -> p m i t", i=PACK),
+                )
+
+        def quantize_w1(chunk, passes, grouped):
+            width = widths[chunk]
+            for n, a in enumerate(passes):
+                group_w1(chunk, a, grouped[:, PACK * width * n : PACK * width * (n + 1)])
+            cols = slice(width * passes[0], width * (passes[-1] + 1))
+            nc.vector.quantize_mx(
+                out=w1_codes[chunk][:, cols].bitcast(FP8X4), scales=w1_scales[chunk][:, cols], in_=grouped
             )
-            n = K_PASSES * b + a
-            nc.vector.quantize_mx(out=w1_codes[n][:].bitcast(FP8X4), scales=w1_scales[n][:], in_=grouped[:])
 
         def load_fresh(t):
-            nc.sync.dma_start(out=dist[t][:], in_=fresh_rows[t // PACK, t % PACK])
+            nc.sync.dma_start(out=dist[t][:], in_=tile_rows(fresh, t))
 
         def load_page(t):
-            if t >= own_pages:
-                page.append(shared.tile([P, T2], F32, name=f"page{t}", offset=4 * T2 * (t - own_pages)))
-            nc.sync.dma_start(out=page[t][:], in_=page_rows[t // PACK, t % PACK])
+            page.append(shared.tile([P, T2], F32, name=f"page{t}", offset=4 * T2 * page_slots[t]))
+            nc.sync.dma_start(out=page[t][:], in_=tile_rows(page0, t))
+
+        def load_gain(i):
+            gain_dealt.append(shared.tile([P, S], F32, name=f"gain{i}", offset=4 * T * 2 + 4 * S * i))
+            for q in range(QUADS):
+                nc.sync.dma_start(out=gain_dealt[i][32 * q : 32 * (q + 1), :], in_=wgs_rows[:, i, :])
 
         def load_expo(t):
-            nc.sync.dma_start(out=exposure[t % PACK][:], in_=expo_rows[t // PACK, t % PACK])
+            nc.sync.dma_start(out=exposure[t][:], in_=tile_rows(expo, t))
 
         def distances(t):
-            b, i = divmod(t, PACK)
-            rows = slice(P * i, P * (i + 1))
+            chunk = min(t // 2, 2)
+            first = P * (t - 2 * chunk)
             for half in range(S // BANK):
                 cols = slice(BANK * half, BANK * (half + 1))
-                bank = banks[(2 * t + half) % len(banks)]
+                unit = 2 * t + half
+                bank, summed, back = (banks[(3 * unit + stage) % len(banks)] for stage in range(3))
                 for a in range(K_PASSES):
-                    n = K_PASSES * b + a
+                    rows = slice(widths[chunk] * a + first, widths[chunk] * a + first + P)
                     nc.tensor.matmul_mx(
                         out=bank[:],
-                        lhsT=w1_codes[n][:, rows].bitcast(FP8X4),
-                        lhsT_scale=w1_scales[n][:, rows],
+                        lhsT=w1_codes[chunk][:, rows].bitcast(FP8X4),
+                        lhsT_scale=w1_scales[chunk][:, rows],
                         rhs=picked[a][:, cols].bitcast(FP8X4),
                         rhs_scale=picked_scales[PACK * a : P, cols],
                         start=(a == 0),
                         stop=(a == K_PASSES - 1),
                     )
-                nc.vector.tensor_tensor(out=dist[t][:, cols], in0=bank[:], in1=dist[t][:, cols], op=ALU.subtract)
-                nc.scalar.activation(out=dist[t][:, cols], in_=dist[t][:, cols], func=ACT.Abs)
+                if t == 0:
+                    nc.vector.tensor_tensor(out=negated[half], in0=bank[:], in1=dist[t][:, cols], op=ALU.subtract)
+                    nc.scalar.activation(out=dist[t][:, cols], in_=negated[half], func=ACT.Abs)
+                    continue
+                nc.scalar.activation(out=negated[half], in_=bank[:], func=ACT.Copy, scale=-1.0)
+                for c in range(BANK // P):
+                    block = slice(P * c, P * (c + 1))
+                    given = dist[t][:, BANK * half + P * c : BANK * half + P * (c + 1)]
+                    nc.tensor.matmul(
+                        out=summed[:, block], lhsT=given, rhs=identity[:], is_transpose=True, start=True, stop=False
+                    )
+                    nc.tensor.matmul(
+                        out=summed[:, block], lhsT=negated[half][:, block], rhs=identity[:],
+                        is_transpose=True, start=False, stop=True,
+                    )
+                nc.scalar.activation(out=turned[half][:], in_=summed[:], func=ACT.Abs)
+                for c in range(BANK // P):
+                    block = slice(P * c, P * (c + 1))
+                    nc.tensor.transpose(back[:, block], turned[half][:, block], identity[:])
+                nc.scalar.copy(out=dist[t][:, cols], in_=back[:])
 
         def put(t, pieces):
-            i = t % PACK
+            gain = gain_plain if t < PACK else gain_dealt[t - PACK]
             width = S // pieces
             for piece in range(pieces):
                 cols = slice(width * piece, width * (piece + 1))
                 entries = idx2[:, width // LIST_COLS * piece : width // LIST_COLS * (piece + 1)]
-                gain = gain_first[:, cols] if i == 0 else gain_rest[:, i - 1, cols]
-                nc.vector.tensor_tensor(out=page[t][:].indirect(entries), in0=dist[t][:, cols], in1=gain, op=ALU.mult)
+                nc.vector.tensor_tensor(out=page[t][:].indirect(entries), in0=dist[t][:, cols], in1=gain[:, cols], op=ALU.mult)
 
         def fetch_x(t):
+            if t < PACK:
+                nc.vector.tensor_tensor(
+                    out=x_plain[t][:], in0=page[t][:].indirect(idx3[:]), in1=exposure[t][:], op=ALU.mult
+                )
+                return
             i = t % PACK
             width = M // 2
             for half in range(2):
@@ -140,84 +190,108 @@ def tile_list_paint_panel_rating_kernel(
                 nc.vector.tensor_tensor(
                     out=x_rows[half][:, i, :],
                     in0=page[t][:].indirect(entries),
-                    in1=exposure[i][:, width * half : width * (half + 1)],
+                    in1=exposure[t][:, width * half : width * (half + 1)],
                     op=ALU.mult,
                 )
 
         def fetch_ref(t):
-            b, i = divmod(t, PACK)
             nc.vector.tensor_copy(out=damp[t][:], in_=page[t][:].indirect(idx4[:]))
-            nc.scalar.activation(out=damp[t][:], in_=damp[t][:], func=ACT.Abs, scale=ref_gain[:, b, i : i + 1])
-            nc.scalar.activation(out=damp[t][:], in_=damp[t][:], func=ACT.Abs_reciprocal_sqrt, bias=1.0)
-            nc.scalar.activation(out=damp[t][:], in_=damp[t][:], func=ACT.Square)
 
-        def quantize_x(b):
-            width = M // 2
+        def damping(t):
+            b, i = divmod(t, PACK)
+            scratch = turned[1]
+            nc.scalar.activation(out=scratch[:], in_=damp[t][:], func=ACT.Abs, scale=ref_gain[b][:, i : i + 1])
+            nc.scalar.activation(out=scratch[:], in_=scratch[:], func=ACT.Abs_reciprocal_sqrt, bias=1.0)
+            nc.scalar.activation(out=damp[t][:], in_=scratch[:], func=ACT.Square)
+
+        def group_x_plain():
+            pairs = shared.tile([P, PACK * M], BF16, name="pairs", offset=4 * T)
+            by_place = pairs[:].rearrange("m (c u p e) -> m c u p e", c=M // P, u=2, e=2)
+            for t in range(PACK):
+                for c in range(M // P):
+                    block = slice(P * c, P * (c + 1))
+                    nc.tensor.transpose(banks[t][:, block], x_plain[t][:, block], identity[:])
+                nc.scalar.copy(
+                    out=by_place[:, :, :, 32 * t : 32 * (t + 1), :],
+                    in_=banks[t][:].rearrange("m (c q u e) -> m c u q e", c=M // P, u=2, e=2),
+                )
+            words = pairs[:].bitcast(F32)
             for half in range(2):
-                views = dict(
-                    out=x_grouped[half][:].rearrange("p (c e i) -> p c i e", e=4, i=PACK),
+                bank = banks[PACK + half]
+                for u in range(2):
+                    for c in range(2):
+                        source = P * (2 * (2 * half + c) + u)
+                        place = P * (2 * u + c)
+                        nc.tensor.transpose(bank[:, place : place + P], words[:, source : source + P], identity[:])
+                nc.scalar.copy(
+                    out=negated[half].rearrange("p (m u) -> p m u", u=2),
+                    in_=bank[:].rearrange("p (u m) -> p m u", u=2),
+                )
+
+        def group_x_dealt():
+            for half, engine_copy in enumerate((nc.scalar.copy, nc.vector.tensor_copy)):
+                engine_copy(
+                    out=negated[half].bitcast(BF16).rearrange("p (c e i) -> p c i e", e=4, i=PACK),
                     in_=x_rows[half][:].rearrange("p i (c e) -> p c i e", e=4),
                 )
-                if b == R_PASSES - 1 and half == 1:
-                    nc.vector.tensor_copy(**views)
-                else:
-                    nc.scalar.copy(**views)
-            for half in range(2):
-                cols = slice(width * half, width * (half + 1))
-                nc.vector.quantize_mx(
-                    out=x_codes[b][:, cols].bitcast(FP8X4), scales=x_scales[b][:, cols], in_=x_grouped[half][:]
-                )
+
+        def quantize_x(b):
+            nc.vector.quantize_mx(out=x_codes[b][:].bitcast(FP8X4), scales=x_scales[b][:], in_=staged[:].bitcast(BF16))
 
         def rate(t, b):
+            i = t % PACK
+            codes = w4_raw[b] if t < PACK else w4_codes[b]
+            planes = w4_scales_raw if t < PACK else w4_planes
             nc.tensor.matmul_mx(
                 out=banks[t][:],
-                lhsT=w4_codes[b][:, 2 * P * t : 2 * P * (t + 1)].bitcast(FP4X4),
-                lhsT_scale=w4_planes[:, b, P * t : P * (t + 1)],
+                lhsT=codes[:, 2 * P * i : 2 * P * (i + 1)].bitcast(FP4X4),
+                lhsT_scale=planes[:, b, P * i : P * (i + 1)],
                 rhs=x_codes[b][:].bitcast(FP8X4),
                 rhs_scale=x_scales[b][:],
                 start=(b == 0),
                 stop=(b == R_PASSES - 1),
             )
 
+        def load_table_scales():
+            for q in range(QUADS):
+                nc.gpsimd.dma_start(
+                    out=table_scales[32 * q : 32 * q + PACK * K_PASSES, :].bitcast(I32),
+                    in_=tab_scales[:, PACK * q : PACK * (q + 1), :].bitcast(I32),
+                )
+
+        def load_w4_scales():
+            for q in range(QUADS):
+                nc.sync.dma_start(
+                    out=w4_scales_raw[32 * q : 32 * q + PACK, :, :].bitcast(I32),
+                    in_=w4_scales[:, PACK * q : PACK * (q + 1), :].rearrange("a r n -> r a n").bitcast(I32),
+                )
+
         nc.vector.memset(table_scales[:].bitcast(I32), 0)
         nc.vector.memset(w4_scales_raw[:].bitcast(I32), 0)
         nc.sync.dma_start(out=idx[:], in_=offs)
         for a in range(K_PASSES):
-            load_w1(0, a)
+            load_w1(a, 0, CHUNK)
             if a == 0:
-                for q in range(QUADS):
-                    nc.sync.dma_start(
-                        out=table_scales[32 * q : 32 * q + PACK * K_PASSES, :].bitcast(I32),
-                        in_=tab_scales[:, PACK * q : PACK * (q + 1), :].bitcast(I32),
-                    )
-                for q in range(QUADS):
-                    nc.sync.dma_start(
-                        out=w4_scales_raw[32 * q : 32 * q + PACK, :, :].bitcast(I32),
-                        in_=w4_scales[:, PACK * q : PACK * (q + 1), :].rearrange("a r n -> r a n").bitcast(I32),
-                    )
+                load_table_scales()
+            if a == K_PASSES - 1:
+                load_w4_scales()
             nc.sync.dma_start(
                 out=table[a][:].bitcast(I32), in_=tab_words[a].rearrange("p t i -> p (t i)").bitcast(I32)
             )
-        nc.sync.dma_start(out=idx2[:], in_=offs2)
-        load_fresh(0)
-        for q in range(QUADS):
-            nc.sync.dma_start(out=gain_first[32 * q : 32 * (q + 1), :], in_=wgs_rows[:, 0, :])
-        load_page(0)
-        load_fresh(1)
-        nc.sync.dma_start(out=idx3[:], in_=offs3)
-        nc.sync.dma_start(out=idx4[:], in_=offs4)
-        load_expo(0)
-        nc.sync.dma_start(out=ref_gain[:], in_=gref.rearrange("(b p i) -> p b i", b=R_PASSES, i=PACK))
-        for q in range(QUADS):
-            nc.sync.dma_start(out=gain_rest[32 * q : 32 * (q + 1), :, :], in_=wgs_rows[:, 1:PACK, :])
+        make_identity(nc, identity[:])
+        nc.gpsimd.memset(gref_rows[:], 0.0)
+        nc.gpsimd.dma_start(out=gref_rows[:PACK, :], in_=gref[:PASS].rearrange("(t p) -> t p", p=P))
+        nc.tensor.transpose(banks[-1][:, :P], gref_rows[:], identity[:])
+        nc.scalar.copy(out=ref_gain[0][:], in_=banks[-1][:, :PACK])
 
         nc.vector.tensor_copy(out=picked_scales[:], in_=table_scales[:].indirect(idx[:]))
-        nc.vector.tensor_copy(
-            out=w4_planes[:].rearrange("p a (b i q) -> p (a b) q i", b=R_PASSES, i=PACK),
-            in_=w4_scales_raw[:].rearrange("p a (b q i) -> p (a b) q i", b=R_PASSES, i=PACK),
-        )
         for a in range(K_PASSES):
-            quantize_w1(0, a)
+            quantize_w1(0, [a], w1_grouped[:, PACK * CHUNK * a : PACK * CHUNK * (a + 1)])
+            if a == K_PASSES - 1:
+                nc.vector.tensor_copy(
+                    out=w4_planes[:].rearrange("p a (i q) -> p a i q", i=PACK),
+                    in_=w4_scales_raw[:, :, PASS:].rearrange("p a (q i) -> p a i q", i=PACK),
+                )
             pieces = 2 if a == K_PASSES - 1 else 1
             width = S // pieces
             for piece in range(pieces):
@@ -226,34 +300,76 @@ def tile_list_paint_panel_rating_kernel(
                     out=picked[a][:, width * piece : width * (piece + 1)], in_=table[a][:].indirect(entries)
                 )
 
+        w1_grouped_last = shared.tile([P, PACK * PASS], BF16, offset=4 * T + 2 * PACK * M, align_bytes=64)
+        nc.sync.dma_start(out=idx2[:], in_=offs2)
+        load_fresh(0)
+        nc.sync.dma_start(out=gain_plain[:, :BANK], in_=wgs[:, :BANK])
+        load_page(0)
+        nc.sync.dma_start(out=gain_plain[:, BANK:], in_=wgs[:, BANK:])
+        load_fresh(1)
+        for a in range(K_PASSES):
+            load_w1(a, CHUNK, CHUNK)
+        nc.sync.dma_start(out=idx3[:], in_=offs3)
+        nc.sync.dma_start(out=idx4[:], in_=offs4)
+        load_expo(0)
+
         distances(0)
         for t in range(TILES):
             if t + 1 < TILES:
-                if t + 2 < TILES:
-                    load_fresh(t + 2)
+                if t == 2:
+                    load_fresh(4)
+                if t >= PACK - 1:
+                    load_gain(t + 1 - PACK)
                 load_page(t + 1)
-                if t < K_PASSES:
-                    load_w1(1, t)
-                    quantize_w1(1, t)
-                if t == K_PASSES:
-                    for b in range(R_PASSES):
-                        nc.sync.dma_start(out=w4_raw[b][:].bitcast(I32), in_=w4_words[b].bitcast(I32))
-                        nc.scalar.copy(
-                            out=w4_codes[b][:].bitcast(U16).rearrange("p (b i q) -> p b q i", b=R_PASSES, i=PACK),
-                            in_=w4_raw[b][:].bitcast(U16).rearrange("p (b q i) -> p b q i", b=R_PASSES, i=PACK),
-                        )
+                if t < 2:
+                    load_fresh(t + 2)
+                elif t + 3 < TILES:
+                    load_fresh(t + 3)
                 distances(t + 1)
+            if t == 0:
+                quantize_w1(1, [0, 1], w1_grouped[:, : 2 * PACK * CHUNK])
+                quantize_w1(1, [2], w1_grouped[:, 2 * PACK * CHUNK : 3 * PACK * CHUNK])
+            if t == 1:
+                for a in range(K_PASSES):
+                    load_w1(a, PASS, PASS)
+                quantize_w1(2, [0, 1], w1_grouped[:])
+                quantize_w1(2, [2], w1_grouped_last[:])
+            if t == PACK - 1:
+                nc.sync.dma_start(out=ref_gain[1][:], in_=gref[PASS:].rearrange("(p i) -> p i", i=PACK))
+                for b in range(R_PASSES):
+                    nc.sync.dma_start(out=w4_raw[b][:].bitcast(I32), in_=w4_words[b].bitcast(I32))
+                    nc.scalar.copy(
+                        out=w4_codes[b][:].bitcast(U16).rearrange("p (i q) -> p i q", i=PACK),
+                        in_=w4_raw[b][:, 2 * PASS :].bitcast(U16).rearrange("p (q i) -> p i q", i=PACK),
+                    )
+            if t == TILES - 2:
+                group_x_plain()
+            if PACK <= t < TILES - 1:
+                damping(2 * (t - PACK))
+                damping(2 * (t - PACK) + 1)
             put(t, 2 if t == 0 else 1)
             fetch_x(t)
             if t + 1 < TILES:
                 load_expo(t + 1)
-            if t % PACK == PACK - 1:
-                quantize_x(t // PACK)
+            if t == TILES - 1:
+                group_x_dealt()
+                quantize_x(1)
             fetch_ref(t)
+            if t == TILES - 2:
+                x_codes[0] = shared.tile([P, M], U32, name="x_codes0", offset=4 * T2 * page_slots[t], align_bytes=64)
+                quantize_x(0)
+            if t >= TILES - 2:
+                damping(t)
 
         for b in range(R_PASSES):
             for t in range(TILES):
                 rate(t, b)
                 if b == R_PASSES - 1:
-                    nc.vector.tensor_tensor(out=damp[t][:], in0=banks[t][:], in1=damp[t][:], op=ALU.mult)
-                    nc.sync.dma_start(out=out_rows[t // PACK, t % PACK], in_=damp[t][:])
+                    pieces = 2 if t == TILES - 1 else 1
+                    width = M // pieces
+                    for piece in range(pieces):
+                        cols = slice(width * piece, width * (piece + 1))
+                        nc.vector.tensor_tensor(
+                            out=damp[t][:, cols], in0=banks[t][:, cols], in1=damp[t][:, cols], op=ALU.mult
+                        )
+                        nc.sync.dma_start(out=tile_rows(out, t)[:, cols], in_=damp[t][:, cols])

from contextlib import ExitStack

import concourse.mybir as mybir
from concourse.masks import make_identity

K, T, S, H, T2, M = 1536, 4096, 1024, 1024, 2048, 512
FLOPS = 2 * K * H * S + 2 * H * H * M

F32 = mybir.dt.float32
BF16 = mybir.dt.bfloat16
I32 = mybir.dt.int32
U32 = mybir.dt.uint32
U16 = mybir.dt.uint16
U8 = mybir.dt.uint8
FP8X4 = mybir.dt.float8_e4m3fn_x4
FP4X4 = mybir.dt.float4_e2m1fn_x4
ACT = mybir.ActivationFunctionType
ALU = mybir.AluOpType

P = 128
PACK = 4
PASS = P * PACK
BANK = 512
K_PASSES = K // PASS
R_PASSES = H // PASS
TILES = H // P
QUADS = 4
LIST_COLS = 16
CHUNK = 2 * P


def tile_list_paint_panel_rating_kernel(
    tc, tab_words, tab_scales, offs, w1, fresh, wgs, page0, offs2, offs3,
    expo, w4_words, w4_scales, offs4, gref, out,
):
    nc = tc.nc

    def tile_rows(matrix, t):
        if t < PACK:
            return matrix[P * t : P * (t + 1), :]
        return matrix[PASS:, :].rearrange("(p i) c -> i p c", i=PACK)[t - PACK]

    wgs_rows = wgs.rearrange("(q i) j -> q i j", i=PACK)

    with ExitStack() as ctx:
        lists = ctx.enter_context(tc.tile_pool(name="lists", bufs=1))
        keep = ctx.enter_context(tc.tile_pool(name="keep", bufs=1))
        shared = ctx.enter_context(tc.tile_pool(name="shared", bufs=1))
        psum = ctx.enter_context(tc.psum_pool(name="psum", bufs=1))

        def tiles(name, count, shape, dtype):
            return [keep.tile(shape, dtype, name=f"{name}{n}", align_bytes=64) for n in range(count)]

        idx = lists.tile([P, S // LIST_COLS], U16, name="idx")
        idx2 = lists.tile([P, S // LIST_COLS], U16, name="idx2")
        idx3 = lists.tile([P, M // LIST_COLS], U16, name="idx3")
        idx4 = lists.tile([P, M // LIST_COLS], U16, name="idx4")

        table = [shared.tile([P, T], U32, name=f"table{a}", offset=4 * T * a) for a in range(K_PASSES)]
        page_slots = [6, 7, 0, 1, 3, 6, 7, 0]
        page = []
        table_scales = keep.tile([P, T], U8, align_bytes=64)
        picked = tiles("picked", K_PASSES, [P, S], U32)
        picked_scales = keep.tile([P, S], U8, align_bytes=64)
        w1_raw = tiles("w1_raw", K_PASSES, [P, PACK, PASS], F32)
        w1_grouped = keep.tile([P, 2 * PACK * PASS], BF16, align_bytes=64)
        widths = (CHUNK, CHUNK, PASS)
        w1_codes = [keep.tile([P, K_PASSES * w], U32, name=f"w1_codes{n}", align_bytes=64) for n, w in enumerate(widths)]
        w1_scales = [keep.tile([P, K_PASSES * w], U8, name=f"w1_scales{n}", align_bytes=64) for n, w in enumerate(widths)]
        gain_plain = keep.tile([P, S], F32, align_bytes=64)
        gain_dealt = []
        identity = keep.tile([P, P], F32, align_bytes=64)
        gref_rows = keep.tile([P, P], F32, align_bytes=64)
        staged = keep.tile([P, 2 * BANK], F32, align_bytes=64)
        negated = [staged[:, BANK * half : BANK * (half + 1)] for half in range(2)]
        turned = tiles("turned", 2, [P, BANK], F32)
        dist = tiles("dist", TILES, [P, S], F32)
        exposure = tiles("exposure", TILES, [P, M], F32)
        x_plain = tiles("x_plain", PACK, [P, M], F32)
        x_rows = tiles("x_rows", 2, [P, PACK, M // 2], F32)
        x_codes = {1: keep.tile([P, M], U32, name="x_codes1", align_bytes=64)}
        x_scales = tiles("x_scales", R_PASSES, [P, M], U8)
        damp = tiles("damp", TILES, [P, M], F32)
        w4_raw = tiles("w4_raw", R_PASSES, [P, 2 * H], U8)
        w4_codes = tiles("w4_codes", R_PASSES, [P, 2 * PASS], U8)
        w4_scales_raw = keep.tile([P, R_PASSES, H], U8, align_bytes=64)
        w4_planes = keep.tile([P, R_PASSES, PASS], U8, align_bytes=64)
        ref_gain = tiles("ref_gain", R_PASSES, [P, PACK], F32)
        banks = [psum.tile([P, BANK], F32, name=f"bank{n}") for n in range(8)]

        def load_w1(a, first, width):
            rows = w1[PASS * a : PASS * (a + 1), first : first + width]
            cols = slice(first % PASS, first % PASS + width)
            nc.sync.dma_start(out=w1_raw[a][:, :, cols], in_=rows.rearrange("(p t) c -> p t c", t=PACK))

        def group_w1(chunk, a, grouped):
            if chunk < 2:
                cols = slice(CHUNK * chunk, CHUNK * (chunk + 1))
                nc.scalar.copy(
                    out=grouped.rearrange("p (c e t) -> p c t e", e=4, t=PACK),
                    in_=w1_raw[a][:, :, cols].rearrange("p t (c e) -> p c t e", e=4),
                )
            else:
                nc.scalar.copy(
                    out=grouped.rearrange("p (i m t) -> p m i t", i=PACK, t=PACK),
                    in_=w1_raw[a][:].rearrange("p t (m i) -> p m i t", i=PACK),
                )

        def quantize_w1(chunk, passes, grouped):
            width = widths[chunk]
            for n, a in enumerate(passes):
                group_w1(chunk, a, grouped[:, PACK * width * n : PACK * width * (n + 1)])
            cols = slice(width * passes[0], width * (passes[-1] + 1))
            nc.vector.quantize_mx(
                out=w1_codes[chunk][:, cols].bitcast(FP8X4), scales=w1_scales[chunk][:, cols], in_=grouped
            )

        def load_fresh(t):
            nc.sync.dma_start(out=dist[t][:], in_=tile_rows(fresh, t))

        def load_page(t):
            page.append(shared.tile([P, T2], F32, name=f"page{t}", offset=4 * T2 * page_slots[t]))
            nc.sync.dma_start(out=page[t][:], in_=tile_rows(page0, t))

        def load_gain(i):
            gain_dealt.append(shared.tile([P, S], F32, name=f"gain{i}", offset=4 * T * 2 + 4 * S * i))
            for q in range(QUADS):
                nc.sync.dma_start(out=gain_dealt[i][32 * q : 32 * (q + 1), :], in_=wgs_rows[:, i, :])

        def load_expo(t):
            nc.sync.dma_start(out=exposure[t][:], in_=tile_rows(expo, t))

        def distances(t):
            chunk = min(t // 2, 2)
            first = P * (t - 2 * chunk)
            for half in range(S // BANK):
                cols = slice(BANK * half, BANK * (half + 1))
                unit = 2 * t + half
                bank, summed, back = (banks[(3 * unit + stage) % len(banks)] for stage in range(3))
                for a in range(K_PASSES):
                    rows = slice(widths[chunk] * a + first, widths[chunk] * a + first + P)
                    nc.tensor.matmul_mx(
                        out=bank[:],
                        lhsT=w1_codes[chunk][:, rows].bitcast(FP8X4),
                        lhsT_scale=w1_scales[chunk][:, rows],
                        rhs=picked[a][:, cols].bitcast(FP8X4),
                        rhs_scale=picked_scales[PACK * a : P, cols],
                        start=(a == 0),
                        stop=(a == K_PASSES - 1),
                    )
                if t == 0:
                    nc.vector.tensor_tensor(out=negated[half], in0=bank[:], in1=dist[t][:, cols], op=ALU.subtract)
                    nc.scalar.activation(out=dist[t][:, cols], in_=negated[half], func=ACT.Abs)
                    continue
                nc.scalar.activation(out=negated[half], in_=bank[:], func=ACT.Copy, scale=-1.0)
                for c in range(BANK // P):
                    block = slice(P * c, P * (c + 1))
                    given = dist[t][:, BANK * half + P * c : BANK * half + P * (c + 1)]
                    nc.tensor.matmul(
                        out=summed[:, block], lhsT=given, rhs=identity[:], is_transpose=True, start=True, stop=False
                    )
                    nc.tensor.matmul(
                        out=summed[:, block], lhsT=negated[half][:, block], rhs=identity[:],
                        is_transpose=True, start=False, stop=True,
                    )
                nc.scalar.activation(out=turned[half][:], in_=summed[:], func=ACT.Abs)
                for c in range(BANK // P):
                    block = slice(P * c, P * (c + 1))
                    nc.tensor.transpose(back[:, block], turned[half][:, block], identity[:])
                nc.scalar.copy(out=dist[t][:, cols], in_=back[:])

        def put(t, pieces):
            gain = gain_plain if t < PACK else gain_dealt[t - PACK]
            width = S // pieces
            for piece in range(pieces):
                cols = slice(width * piece, width * (piece + 1))
                entries = idx2[:, width // LIST_COLS * piece : width // LIST_COLS * (piece + 1)]
                nc.vector.tensor_tensor(out=page[t][:].indirect(entries), in0=dist[t][:, cols], in1=gain[:, cols], op=ALU.mult)

        def fetch_x(t):
            if t < PACK:
                nc.vector.tensor_tensor(
                    out=x_plain[t][:], in0=page[t][:].indirect(idx3[:]), in1=exposure[t][:], op=ALU.mult
                )
                return
            i = t % PACK
            width = M // 2
            for half in range(2):
                entries = idx3[:, width // LIST_COLS * half : width // LIST_COLS * (half + 1)]
                nc.vector.tensor_tensor(
                    out=x_rows[half][:, i, :],
                    in0=page[t][:].indirect(entries),
                    in1=exposure[t][:, width * half : width * (half + 1)],
                    op=ALU.mult,
                )

        def fetch_ref(t):
            nc.vector.tensor_copy(out=damp[t][:], in_=page[t][:].indirect(idx4[:]))

        def damping(t):
            b, i = divmod(t, PACK)
            scratch = turned[1]
            nc.scalar.activation(out=scratch[:], in_=damp[t][:], func=ACT.Abs, scale=ref_gain[b][:, i : i + 1])
            nc.scalar.activation(out=scratch[:], in_=scratch[:], func=ACT.Abs_reciprocal_sqrt, bias=1.0)
            nc.scalar.activation(out=damp[t][:], in_=scratch[:], func=ACT.Square)

        def group_x_plain():
            pairs = shared.tile([P, PACK * M], BF16, name="pairs", offset=4 * T)
            by_place = pairs[:].rearrange("m (c u p e) -> m c u p e", c=M // P, u=2, e=2)
            for t in range(PACK):
                for c in range(M // P):
                    block = slice(P * c, P * (c + 1))
                    nc.tensor.transpose(banks[t][:, block], x_plain[t][:, block], identity[:])
                nc.scalar.copy(
                    out=by_place[:, :, :, 32 * t : 32 * (t + 1), :],
                    in_=banks[t][:].rearrange("m (c q u e) -> m c u q e", c=M // P, u=2, e=2),
                )
            words = pairs[:].bitcast(F32)
            for half in range(2):
                bank = banks[PACK + half]
                for u in range(2):
                    for c in range(2):
                        source = P * (2 * (2 * half + c) + u)
                        place = P * (2 * u + c)
                        nc.tensor.transpose(bank[:, place : place + P], words[:, source : source + P], identity[:])
                nc.scalar.copy(
                    out=negated[half].rearrange("p (m u) -> p m u", u=2),
                    in_=bank[:].rearrange("p (u m) -> p m u", u=2),
                )

        def group_x_dealt():
            for half, engine_copy in enumerate((nc.scalar.copy, nc.vector.tensor_copy)):
                engine_copy(
                    out=negated[half].bitcast(BF16).rearrange("p (c e i) -> p c i e", e=4, i=PACK),
                    in_=x_rows[half][:].rearrange("p i (c e) -> p c i e", e=4),
                )

        def quantize_x(b):
            nc.vector.quantize_mx(out=x_codes[b][:].bitcast(FP8X4), scales=x_scales[b][:], in_=staged[:].bitcast(BF16))

        def rate(t, b):
            i = t % PACK
            codes = w4_raw[b] if t < PACK else w4_codes[b]
            planes = w4_scales_raw if t < PACK else w4_planes
            nc.tensor.matmul_mx(
                out=banks[t][:],
                lhsT=codes[:, 2 * P * i : 2 * P * (i + 1)].bitcast(FP4X4),
                lhsT_scale=planes[:, b, P * i : P * (i + 1)],
                rhs=x_codes[b][:].bitcast(FP8X4),
                rhs_scale=x_scales[b][:],
                start=(b == 0),
                stop=(b == R_PASSES - 1),
            )

        def load_table_scales():
            for q in range(QUADS):
                nc.gpsimd.dma_start(
                    out=table_scales[32 * q : 32 * q + PACK * K_PASSES, :].bitcast(I32),
                    in_=tab_scales[:, PACK * q : PACK * (q + 1), :].bitcast(I32),
                )

        def load_w4_scales():
            for q in range(QUADS):
                nc.sync.dma_start(
                    out=w4_scales_raw[32 * q : 32 * q + PACK, :, :].bitcast(I32),
                    in_=w4_scales[:, PACK * q : PACK * (q + 1), :].rearrange("a r n -> r a n").bitcast(I32),
                )

        nc.vector.memset(table_scales[:].bitcast(I32), 0)
        nc.vector.memset(w4_scales_raw[:].bitcast(I32), 0)
        nc.sync.dma_start(out=idx[:], in_=offs)
        for a in range(K_PASSES):
            load_w1(a, 0, CHUNK)
            if a == 0:
                load_table_scales()
            if a == K_PASSES - 1:
                load_w4_scales()
            nc.sync.dma_start(
                out=table[a][:].bitcast(I32), in_=tab_words[a].rearrange("p t i -> p (t i)").bitcast(I32)
            )
        make_identity(nc, identity[:])
        nc.gpsimd.memset(gref_rows[:], 0.0)
        nc.gpsimd.dma_start(out=gref_rows[:PACK, :], in_=gref[:PASS].rearrange("(t p) -> t p", p=P))
        nc.tensor.transpose(banks[-1][:, :P], gref_rows[:], identity[:])
        nc.scalar.copy(out=ref_gain[0][:], in_=banks[-1][:, :PACK])

        nc.vector.tensor_copy(out=picked_scales[:], in_=table_scales[:].indirect(idx[:]))
        for a in range(K_PASSES):
            quantize_w1(0, [a], w1_grouped[:, PACK * CHUNK * a : PACK * CHUNK * (a + 1)])
            if a == K_PASSES - 1:
                nc.vector.tensor_copy(
                    out=w4_planes[:].rearrange("p a (i q) -> p a i q", i=PACK),
                    in_=w4_scales_raw[:, :, PASS:].rearrange("p a (q i) -> p a i q", i=PACK),
                )
            pieces = 2 if a == K_PASSES - 1 else 1
            width = S // pieces
            for piece in range(pieces):
                entries = idx[:, width // LIST_COLS * piece : width // LIST_COLS * (piece + 1)]
                nc.vector.tensor_copy(
                    out=picked[a][:, width * piece : width * (piece + 1)], in_=table[a][:].indirect(entries)
                )

        w1_grouped_last = shared.tile([P, PACK * PASS], BF16, offset=4 * T + 2 * PACK * M, align_bytes=64)
        nc.sync.dma_start(out=idx2[:], in_=offs2)
        load_fresh(0)
        nc.sync.dma_start(out=gain_plain[:, :BANK], in_=wgs[:, :BANK])
        load_page(0)
        nc.sync.dma_start(out=gain_plain[:, BANK:], in_=wgs[:, BANK:])
        load_fresh(1)
        for a in range(K_PASSES):
            load_w1(a, CHUNK, CHUNK)
        nc.sync.dma_start(out=idx3[:], in_=offs3)
        nc.sync.dma_start(out=idx4[:], in_=offs4)
        load_expo(0)

        distances(0)
        for t in range(TILES):
            if t + 1 < TILES:
                if t == 2:
                    load_fresh(4)
                if t >= PACK - 1:
                    load_gain(t + 1 - PACK)
                load_page(t + 1)
                if t < 2:
                    load_fresh(t + 2)
                elif t + 3 < TILES:
                    load_fresh(t + 3)
                distances(t + 1)
            if t == 0:
                quantize_w1(1, [0, 1], w1_grouped[:, : 2 * PACK * CHUNK])
                quantize_w1(1, [2], w1_grouped[:, 2 * PACK * CHUNK : 3 * PACK * CHUNK])
            if t == 1:
                for a in range(K_PASSES):
                    load_w1(a, PASS, PASS)
                quantize_w1(2, [0, 1], w1_grouped[:])
                quantize_w1(2, [2], w1_grouped_last[:])
            if t == PACK - 1:
                nc.sync.dma_start(out=ref_gain[1][:], in_=gref[PASS:].rearrange("(p i) -> p i", i=PACK))
                for b in range(R_PASSES):
                    nc.sync.dma_start(out=w4_raw[b][:].bitcast(I32), in_=w4_words[b].bitcast(I32))
                    nc.scalar.copy(
                        out=w4_codes[b][:].bitcast(U16).rearrange("p (i q) -> p i q", i=PACK),
                        in_=w4_raw[b][:, 2 * PASS :].bitcast(U16).rearrange("p (q i) -> p i q", i=PACK),
                    )
            if t == TILES - 2:
                group_x_plain()
            if PACK <= t < TILES - 1:
                damping(2 * (t - PACK))
                damping(2 * (t - PACK) + 1)
            put(t, 2 if t == 0 else 1)
            fetch_x(t)
            if t + 1 < TILES:
                load_expo(t + 1)
            if t == TILES - 1:
                group_x_dealt()
                quantize_x(1)
            fetch_ref(t)
            if t == TILES - 2:
                x_codes[0] = shared.tile([P, M], U32, name="x_codes0", offset=4 * T2 * page_slots[t], align_bytes=64)
                quantize_x(0)
            if t >= TILES - 2:
                damping(t)

        for b in range(R_PASSES):
            for t in range(TILES):
                rate(t, b)
                if b == R_PASSES - 1:
                    pieces = 2 if t == TILES - 1 else 1
                    width = M // pieces
                    for piece in range(pieces):
                        cols = slice(width * piece, width * (piece + 1))
                        nc.vector.tensor_tensor(
                            out=damp[t][:, cols], in0=banks[t][:, cols], in1=damp[t][:, cols], op=ALU.mult
                        )
                        nc.sync.dma_start(out=tile_rows(out, t)[:, cols], in_=damp[t][:, cols])
